import numpy as np
import ml_dtypes


def mxq(x, axis, fmt="e4m3"):
    dtype, down = {"e4m3": (ml_dtypes.float8_e4m3fn, 7), "e5m2": (ml_dtypes.float8_e5m2, 14)}[fmt]
    v = np.moveaxis(np.asarray(x, np.float32).astype(ml_dtypes.bfloat16).astype(np.float64), axis, -1)
    blocks = v.reshape(v.shape[:-1] + (-1, 32))
    amax = np.abs(blocks).max(-1, keepdims=True)
    byte = np.maximum(np.where(amax > 0, np.frexp(amax)[1] - 1 + 127, 0) - down, 1)
    scale = np.exp2(byte - 127.0)
    codes = (blocks / scale).astype(np.float32).astype(dtype).astype(np.float64)
    return np.moveaxis((codes * scale).reshape(v.shape), -1, axis)


WIDE = False


def mx_kscale(k):
    if not WIDE:
        return np.ones(k)
    levels = np.array([10, -10, 5, -5, 0])
    if k % 512:
        return np.exp2(np.random.permutation(np.resize(levels, k // 32))).repeat(32)
    a = np.empty((k // 512, 16))
    for p in range(k // 512):
        a[p, :8] = np.random.permutation(np.resize(levels, 8))
        for g in range(8):
            far = levels[np.abs(levels - a[p, g]) >= 10]
            a[p, g + 8] = far[np.random.randint(len(far))]
    return np.exp2(a.ravel()).repeat(32)


def f64(x):
    return np.asarray(x).astype(np.float64)


def striped(idx):
    return np.tile(idx.reshape(-1, 16).T, (8, 1)).astype(np.uint16)


def unstriped(offs):
    return offs[:16].T.reshape(-1).astype(np.int64)


def striped8(idx):
    return np.concatenate([x.reshape(-1, 16).T for x in idx]).astype(np.uint16)


def runs(offs, k):
    lists = np.stack([offs[16 * r : 16 * r + 16].T.reshape(-1) for r in range(8)]).astype(np.int64)
    return lists[np.arange(k) % 512 // 64]


def pack_weight(w):
    k, n = w.shape
    w = f64(np.asarray(w, np.float32).astype(ml_dtypes.bfloat16)).reshape(k // 32, 32, n)
    amax = np.abs(w).max(1)
    byte = np.clip(np.where(amax > 0, np.frexp(amax)[1] - 1 + 127 - 7, 1), 1, 254)
    scaled = (w * np.exp2(127.0 - byte)[:, None, :]).reshape(k, n).astype(np.float32)
    words = np.ascontiguousarray(scaled.reshape(k // 512, 128, 4, n).transpose(0, 1, 3, 2)).astype(ml_dtypes.float8_e4m3fn).view(np.uint8)
    return words, np.ascontiguousarray(byte.astype(np.uint8).reshape(k // 512, 16, n))


def unpack_weight(words, scales):
    g, p, n, _ = words.shape
    vals = np.ascontiguousarray(words).view(ml_dtypes.float8_e4m3fn).astype(np.float64) * np.repeat(np.exp2(scales.astype(np.float64) - 127.0), 8, axis=1)[..., None]
    return vals.transpose(0, 1, 3, 2).reshape(g * 512, n)


def sigmoid(v):
    return 1.0 / (1.0 + np.exp(-np.maximum(v, -700.0)))


K, T, S, N, H = 512, 2048, 512, 512, 512


def setup_inputs():
    n = np.random.standard_normal
    s = mx_kscale(K)[:, None]
    u = mx_kscale(S)
    packed_xT = pack_weight(n((K, T)) * s)
    return {
        "x_words": packed_xT[0],
        "x_scales": packed_xT[1],
        "wa": (n((K, H)) / np.sqrt(K) / s).astype(np.float32),
        "wb": (n((K, N)) / np.sqrt(K) / s).astype(np.float32),
        "gt": (np.random.uniform(0.5, 1.5, (S, 1)) * u[:, None]).astype(np.float32),
        "gi": (np.random.uniform(0.5, 1.5, (S, 1)) / u[:, None]).astype(np.float32),
        "offs": striped(np.random.permutation(T)[:S]),
        "two": striped(np.random.permutation(T)[:S]),
        "n1": striped8(np.stack([np.random.permutation(H) for _ in range(8)])),
        "n2": striped8(np.stack([np.random.permutation(H) for _ in range(8)])),
        "n3": striped8(np.stack([np.random.permutation(N) for _ in range(8)])),
        "n4": striped8(np.stack([np.random.permutation(N) for _ in range(8)])),
        "n5": striped8(np.stack([np.random.permutation(N) for _ in range(8)])),
        "n6": striped8(np.stack([np.random.permutation(N) for _ in range(8)])),
        "n7": striped8(np.stack([np.random.permutation(N) for _ in range(8)])),
    }


def reference(x_words, x_scales, wa, wb, gt, gi, offs, two, n1, n2, n3, n4, n5, n6, n7):
    xq = unpack_weight(x_words, x_scales)[:, unstriped(offs)]
    a = xq.T @ mxq(f64(wa), 0, "e4m3")
    z = f64(gt) * (np.maximum(a * (sigmoid(a[np.arange(S)[:, None], runs(n1, S)])), a[np.arange(S)[:, None], runs(n2, S)]))
    x_two = unpack_weight(x_words, x_scales)[:, unstriped(two)]
    b = x_two.T @ mxq(f64(wb), 0, "e4m3")
    z2 = f64(gi) * (np.minimum(np.maximum(b, b[np.arange(S)[:, None], runs(n3, S)]), b[np.arange(S)[:, None], runs(n4, S)]))
    cv = 0.0625 * ((mxq(z, 0, "e4m3").T @ mxq(z2, 0, "e4m3")))
    return (cv[np.arange(H)[:, None], runs(n5, H)]) * sigmoid(cv) + (cv[np.arange(H)[:, None], runs(n6, H)]) * (sigmoid(cv[np.arange(H)[:, None], runs(n7, H)]))

@@ -1,0 +1,248 @@
+from contextlib import ExitStack
+
+import concourse.mybir as mybir
+from concourse.masks import make_identity
+
+K, T, S, H, N = 512, 2048, 512, 512, 512
+FLOPS = 3 * 2 * 512 * 512 * 512
+
+F32 = mybir.dt.float32
+BF16 = mybir.dt.bfloat16
+I32 = mybir.dt.int32
+U32 = mybir.dt.uint32
+U16 = mybir.dt.uint16
+U8 = mybir.dt.uint8
+FP8X4 = mybir.dt.float8_e4m3fn_x4
+ALU = mybir.AluOpType
+ACT = mybir.ActivationFunctionType
+
+P = 128
+PACK = 4
+WINDOW = 1024
+
+
+def tile_picked_mombgmaxminmxwsum_none_p_kernel(
+    tc, x_words, x_scales, wa, wb, gt, gi, offs, two, n1, n2, n3, n4, n5, n6, n7, out
+):
+    nc = tc.nc
+    with ExitStack() as ctx:
+        keep = ctx.enter_context(tc.tile_pool(name="keep", bufs=1))
+        psum = ctx.enter_context(tc.psum_pool(name="psum", bufs=1))
+
+        def load_list(src, name):
+            tile = keep.tile([P, S // 16], U16, name=name)
+            nc.sync.dma_start(tile[:], src)
+            return tile
+
+        def load_weight_half(w, half, name):
+            tile = keep.tile([P, PACK, 256], F32, name=name)
+            nc.sync.dma_start(tile[:], w.rearrange("(p j) c -> p j c", j=PACK)[:, :, 256 * half : 256 * (half + 1)])
+            return tile
+
+        table_scales = keep.tile([P, T], U8, name="table_scales")
+        nc.gpsimd.memset(table_scales[:].bitcast(I32), 0)
+        gate_rows = keep.tile([P, P + 8], F32, name="gate_rows")
+        nc.gpsimd.memset(gate_rows[:], 0.0)
+        identity = keep.tile([P, P], F32, name="identity")
+        make_identity(nc, identity[:])
+
+        warm = keep.tile([P, 1], F32, name="warm")
+        two_t = load_list(two, "two_t")
+        offs_t = load_list(offs, "offs_t")
+        for q in range(4):
+            nc.scalar.dma_start(
+                table_scales[32 * q : 32 * q + 4, :].bitcast(I32), x_scales[0, 4 * q : 4 * q + 4, :].bitcast(I32)
+            )
+        nc.scalar.activation(warm[:], gate_rows[:, P : P + 1], ACT.Sigmoid)
+        wb_raw = [load_weight_half(wb, half, "wb_raw%d" % half) for half in range(2)]
+        table_words = keep.tile([P, T], I32, name="table_words")
+        nc.sync.dma_start(table_words[:], x_words[0].rearrange("p n t -> p (n t)").bitcast(I32))
+        wa_raw = [load_weight_half(wa, half, "wa_raw%d" % half) for half in range(2)]
+        n3_t = load_list(n3, "n3_t")
+        n4_t = load_list(n4, "n4_t")
+        for row, gate in ((0, gi), (4, gt)):
+            nc.sync.dma_start(
+                gate_rows[row : row + 4, 0:P].rearrange("t (g e) -> t g e", e=4),
+                gate.rearrange("(g t e) o -> t g (e o)", t=4, e=4),
+            )
+        n1_t = load_list(n1, "n1_t")
+        n2_t = load_list(n2, "n2_t")
+        n5_t = load_list(n5, "n5_t")
+        n6_t = load_list(n6, "n6_t")
+        n7_t = load_list(n7, "n7_t")
+        gate_ps = psum.tile([P, P], F32, name="gate_ps", tag="bank7")
+        nc.tensor.transpose(gate_ps[:], gate_rows[:, 0:P], identity[:])
+        gates = keep.tile([P, 8], F32, name="gates")
+        nc.scalar.activation(gates[:], gate_ps[:, 0:8], ACT.Copy)
+
+        def gather_words(lst, name):
+            words = keep.tile([P, S], U32, name=name, align_bytes=64)
+            nc.vector.tensor_copy(
+                words[:].rearrange("p (t g e) -> p g t e", t=4, e=4),
+                table_words[:].bitcast(U32).indirect(lst[:]),
+            )
+            return words
+
+        def gather_scales(lst, name):
+            listed = keep.tile([P, S], U8, name=name + "_listed")
+            nc.vector.tensor_copy(listed[:], table_scales[:].indirect(lst[:]))
+            return listed
+
+        def deal_scales(listed, name):
+            dealt = keep.tile([P, S], U8, name=name, align_bytes=64)
+            nc.vector.tensor_copy(
+                dealt[:].bitcast(I32).rearrange("p (t g) -> p t g", t=4),
+                listed[:].bitcast(I32).rearrange("p (g t) -> p t g", t=4),
+            )
+            return dealt
+
+        def interleave_weight(raw, name):
+            grouped = keep.tile([P, PACK * 512], BF16, name=name, tag=name, align_bytes=64)
+            for half in range(2):
+                nc.scalar.copy(
+                    grouped[:, 1024 * half : 1024 * (half + 1)].rearrange("p (c i j) -> p c j i", i=4, j=PACK),
+                    raw[half][:].rearrange("p j (c i) -> p c j i", i=4),
+                )
+            return grouped
+
+        def quantize(grouped, name):
+            codes = keep.tile([P, 512], U32, name=name + "_codes", align_bytes=64)
+            scales = keep.tile([P, 512], U8, name=name + "_scales", align_bytes=64)
+            nc.vector.quantize_mx(out=codes[:].bitcast(FP8X4), scales=scales[:], in_=grouped[:])
+            return codes, scales
+
+        def product(bank, lhs_codes, lhs_scales, t, rhs_codes, rhs_scales):
+            cols = slice(P * t, P * (t + 1))
+            nc.tensor.matmul_mx(
+                out=bank[:],
+                lhsT=lhs_codes[:, cols].bitcast(FP8X4),
+                lhsT_scale=lhs_scales[:, cols],
+                rhs=rhs_codes[:].bitcast(FP8X4),
+                rhs_scale=rhs_scales[:],
+                start=True,
+                stop=True,
+            )
+
+        def work(name, tag=None):
+            return keep.tile([P, 512], F32, name=name, tag=tag or name, align_bytes=64)
+
+        xb_listed = gather_scales(two_t, "xb_scales")
+        xa_listed = gather_scales(offs_t, "xa_scales")
+        xb_scales = deal_scales(xb_listed, "xb_scales")
+        xa_scales = deal_scales(xa_listed, "xa_scales")
+        wb_grouped = interleave_weight(wb_raw, "wb_grouped")
+        wb_codes, wb_scales = quantize(wb_grouped, "wb")
+        xb_words = gather_words(two_t, "xb_words")
+        xa_words = gather_words(offs_t, "xa_words")
+
+        b_banks = [psum.tile([P, 512], F32, name="b_bank%d" % t, tag="bank%d" % t) for t in range(4)]
+        b_win = [keep.tile([P, WINDOW], F32, name="b_win%d" % t) for t in range(4)]
+        for t in range(4):
+            product(b_banks[t], xb_words, xb_scales, t, wb_codes, wb_scales)
+            nc.scalar.activation(b_win[t][:, 0:512], b_banks[t][:], ACT.Copy)
+            if t == 1:
+                wa_grouped = interleave_weight(wa_raw, "wa_grouped")
+
+        z2_grouped = keep.tile([P, PACK * 512], BF16, name="z2_grouped", align_bytes=64)
+        z_grouped = keep.tile([P, PACK * 512], BF16, name="z_grouped", align_bytes=64)
+        a_banks = [psum.tile([P, 512], F32, name="a_bank%d" % t, tag="bank%d" % (4 + t)) for t in range(4)]
+        a_win = [keep.tile([P, WINDOW], F32, name="a_win%d" % t) for t in range(4)]
+        sig1 = [work("sig1_%d" % t) for t in range(4)]
+
+        g3_tags = ["slot0", "wa_grouped", "slot1", "slot2"]
+        g4_tags = ["slot1", "slot2", "wa_grouped", "slot1"]
+
+        def b_gathers(t):
+            g3 = work("g3_%d" % t, g3_tags[t])
+            nc.vector.tensor_copy(g3[:], b_win[t][:].indirect(n3_t[:]))
+            g4 = work("g4_%d" % t, g4_tags[t])
+            nc.vector.tensor_copy(g4[:], b_win[t][:].indirect(n4_t[:]))
+            return g3, g4
+
+        def a_start(t):
+            product(a_banks[t], xa_words, xa_scales, t, wa_codes, wa_scales)
+            nc.scalar.activation(a_win[t][:, 0:512], a_banks[t][:], ACT.Copy)
+            nc.scalar.activation(sig1[t][:], a_win[t][:].indirect(n1_t[:]), ACT.Sigmoid)
+
+        def a_gather(t):
+            g2 = work("g2_%d" % t)
+            nc.vector.tensor_copy(g2[:], a_win[t][:].indirect(n2_t[:]))
+            return g2
+
+        g3, g4 = b_gathers(0)
+        for t in range(4):
+            upper = work("upper%d" % t)
+            nc.vector.tensor_tensor(upper[:], b_banks[t][:], g3[:], ALU.max)
+            if t == 0:
+                wa_codes, wa_scales = quantize(wa_grouped, "wa")
+            a_start(t)
+            this_g4 = g4
+            if t < 3:
+                g3, g4 = b_gathers(t + 1)
+                low = b_win[t + 1][:, 512:WINDOW]
+            else:
+                g2 = a_gather(0)
+                low = a_win[0][:, 512:WINDOW]
+            nc.vector.tensor_tensor(low, upper[:], this_g4[:], ALU.min)
+            nc.scalar.activation(
+                z2_grouped[:].rearrange("p (c t) -> p c t", t=4)[:, :, t], low, ACT.Copy, scale=gates[:, t : t + 1]
+            )
+
+        z_codes = keep.tile([P, 512], U32, name="z_codes", align_bytes=64)
+        z_scales = keep.tile([P, 512], U8, name="z_scales", align_bytes=64)
+
+        for t in range(4):
+            gated = work("gated%d" % t)
+            nc.vector.tensor_tensor(gated[:], a_banks[t][:], sig1[t][:], ALU.mult)
+            this_g2 = g2
+            if t < 3:
+                g2 = a_gather(t + 1)
+            if t == 2:
+                z2_codes, z2_scales = quantize(z2_grouped, "z2")
+            larger = a_win[t + 1][:, 512:WINDOW] if t < 3 else b_win[0][:, 512:WINDOW]
+            nc.vector.tensor_tensor(larger, gated[:], this_g2[:], ALU.max)
+            gate_col = gates[:, 4 + t : 5 + t]
+            if t < 3:
+                nc.scalar.activation(
+                    z_grouped[:].rearrange("p (u m t) -> p m u t", u=4, t=4)[:, :, :, t],
+                    larger.rearrange("p (m u) -> p m u", u=4),
+                    ACT.Copy,
+                    scale=gate_col,
+                )
+            else:
+                for u in range(4):
+                    piece = z_grouped[:, 512 * u : 512 * (u + 1)]
+                    nc.scalar.activation(
+                        piece.rearrange("p (m t) -> p m t", t=4)[:, :, t],
+                        larger.rearrange("p (m u) -> p m u", u=4)[:, :, u],
+                        ACT.Copy,
+                        scale=gate_col,
+                    )
+                    cols = slice(P * u, P * (u + 1))
+                    nc.vector.quantize_mx(out=z_codes[:, cols].bitcast(FP8X4), scales=z_scales[:, cols], in_=piece)
+
+        out_rows = out.rearrange("(m u) n -> m u n", u=4)
+
+        def finish(u, first, second, tag):
+            total = work("total%d" % u, tag)
+            nc.vector.tensor_tensor(total[:], first[:], second[:], ALU.add)
+            nc.sync.dma_start(out_rows[:, u, :], total[:])
+
+        pending = None
+        for u in range(4):
+            bank = psum.tile([P, 512], F32, name="cv_bank%d" % u, tag="bank%d" % u)
+            product(bank, z_codes, z_scales, u, z2_codes, z2_scales)
+            cv_win = keep.tile([P, WINDOW], F32, name="cv_win%d" % u)
+            nc.scalar.activation(cv_win[:, 0:512], bank[:], ACT.Copy, scale=0.0625)
+            sig_here = work("sig_here%d" % u)
+            nc.scalar.activation(sig_here[:], bank[:], ACT.Sigmoid, scale=0.0625)
+            sig7 = work("sig7_%d" % u)
+            nc.scalar.activation(sig7[:], cv_win[:].indirect(n7_t[:]), ACT.Sigmoid)
+            first = work("first%d" % u)
+            nc.vector.tensor_tensor(first[:], cv_win[:].indirect(n5_t[:]), sig_here[:], ALU.mult)
+            if pending:
+                finish(*pending, "sig_here%d" % u)
+            second = work("second%d" % u)
+            nc.vector.tensor_tensor(second[:], cv_win[:].indirect(n6_t[:]), sig7[:], ALU.mult)
+            pending = (u, first, second)
+        finish(*pending, None)

@@ -57,7 +57,6 @@ def tile_picked_mombgmaxminmxwsum_none_p_kernel(
         wb_raw = [load_weight_half(wb, half, "wb_raw%d" % half) for half in range(2)]
         table_words = keep.tile([P, T], I32, name="table_words")
         nc.sync.dma_start(table_words[:], x_words[0].rearrange("p n t -> p (n t)").bitcast(I32))
-        wa_raw = [load_weight_half(wa, half, "wa_raw%d" % half) for half in range(2)]
         n3_t = load_list(n3, "n3_t")
         n4_t = load_list(n4, "n4_t")
         for row, gate in ((0, gi), (4, gt)):
@@ -65,6 +64,7 @@ def tile_picked_mombgmaxminmxwsum_none_p_kernel(
                 gate_rows[row : row + 4, 0:P].rearrange("t (g e) -> t g e", e=4),
                 gate.rearrange("(g t e) o -> t g (e o)", t=4, e=4),
             )
+        wa_raw = [load_weight_half(wa, half, "wa_raw%d" % half) for half in range(2)]
         n1_t = load_list(n1, "n1_t")
         n2_t = load_list(n2, "n2_t")
         n5_t = load_list(n5, "n5_t")
@@ -74,6 +74,14 @@ def tile_picked_mombgmaxminmxwsum_none_p_kernel(
         nc.tensor.transpose(gate_ps[:], gate_rows[:, 0:P], identity[:])
         gates = keep.tile([P, 8], F32, name="gates")
         nc.scalar.activation(gates[:], gate_ps[:, 0:8], ACT.Copy)
+        gt_size = keep.tile([P, 4], F32, name="gt_size")
+        nc.scalar.activation(gt_size[:], gate_ps[:, 4:8], ACT.Abs)
+        gt_step = keep.tile([P, 4], F32, name="gt_step")
+        nc.gpsimd.tensor_scalar(gt_step[:], gates[:, 4:8], 0.0, 2.0, ALU.is_ge, ALU.mult)
+        gt_sign = keep.tile([P, 4], F32, name="gt_sign")
+        nc.gpsimd.tensor_scalar(gt_sign[:], gt_step[:], 1.0, -1.0, ALU.mult, ALU.add)
+        gi_signed = keep.tile([P, 4], F32, name="gi_signed")
+        nc.gpsimd.tensor_tensor(gi_signed[:], gates[:, 0:4], gt_sign[:], ALU.mult)
 
         def gather_words(lst, name):
             words = keep.tile([P, S], U32, name=name, align_bytes=64)
@@ -100,8 +108,8 @@ def tile_picked_mombgmaxminmxwsum_none_p_kernel(
             grouped = keep.tile([P, PACK * 512], BF16, name=name, tag=name, align_bytes=64)
             for half in range(2):
                 nc.scalar.copy(
-                    grouped[:, 1024 * half : 1024 * (half + 1)].rearrange("p (c i j) -> p c j i", i=4, j=PACK),
-                    raw[half][:].rearrange("p j (c i) -> p c j i", i=4),
+                    grouped[:, 1024 * half : 1024 * (half + 1)].rearrange("p (c i j) -> p c j i", i=2, j=PACK),
+                    raw[half][:].rearrange("p j (c i) -> p c j i", i=2),
                 )
             return grouped
 
@@ -143,10 +151,12 @@ def tile_picked_mombgmaxminmxwsum_none_p_kernel(
             if t == 1:
                 wa_grouped = interleave_weight(wa_raw, "wa_grouped")
 
-        z2_grouped = keep.tile([P, PACK * 512], BF16, name="z2_grouped", align_bytes=64)
-        z_grouped = keep.tile([P, PACK * 512], BF16, name="z_grouped", align_bytes=64)
+        z2_rows = keep.tile([P, 4, 512], F32, name="z2_rows")
         a_banks = [psum.tile([P, 512], F32, name="a_bank%d" % t, tag="bank%d" % (4 + t)) for t in range(4)]
         a_win = [keep.tile([P, WINDOW], F32, name="a_win%d" % t) for t in range(4)]
+        a_scaled = [keep.tile([P, WINDOW], F32, name="a_scaled%d" % t) for t in range(4)]
+        gated = keep.tile([P, 4, 512], F32, name="gated")
+        g2 = keep.tile([P, 4, 512], F32, name="g2")
         sig1 = [work("sig1_%d" % t) for t in range(4)]
 
         g3_tags = ["slot0", "wa_grouped", "slot1", "slot2"]
@@ -161,13 +171,12 @@ def tile_picked_mombgmaxminmxwsum_none_p_kernel(
 
         def a_start(t):
             product(a_banks[t], xa_words, xa_scales, t, wa_codes, wa_scales)
+            nc.scalar.activation(a_scaled[t][:, 0:512], a_banks[t][:], ACT.Copy, scale=gt_size[:, t : t + 1])
             nc.scalar.activation(a_win[t][:, 0:512], a_banks[t][:], ACT.Copy)
             nc.scalar.activation(sig1[t][:], a_win[t][:].indirect(n1_t[:]), ACT.Sigmoid)
 
         def a_gather(t):
-            g2 = work("g2_%d" % t)
-            nc.vector.tensor_copy(g2[:], a_win[t][:].indirect(n2_t[:]))
-            return g2
+            nc.vector.tensor_copy(g2[:, t, :], a_scaled[t][:].indirect(n2_t[:]))
 
         g3, g4 = b_gathers(0)
         for t in range(4):
@@ -175,64 +184,70 @@ def tile_picked_mombgmaxminmxwsum_none_p_kernel(
             nc.vector.tensor_tensor(upper[:], b_banks[t][:], g3[:], ALU.max)
             if t == 0:
                 wa_codes, wa_scales = quantize(wa_grouped, "wa")
-            a_start(t)
+                for s in range(4):
+                    a_start(s)
             this_g4 = g4
             if t < 3:
                 g3, g4 = b_gathers(t + 1)
                 low = b_win[t + 1][:, 512:WINDOW]
             else:
-                g2 = a_gather(0)
-                low = a_win[0][:, 512:WINDOW]
+                a_gather(0)
+                low = a_scaled[0][:, 512:WINDOW]
             nc.vector.tensor_tensor(low, upper[:], this_g4[:], ALU.min)
-            nc.scalar.activation(
-                z2_grouped[:].rearrange("p (c t) -> p c t", t=4)[:, :, t], low, ACT.Copy, scale=gates[:, t : t + 1]
+            nc.scalar.activation(z2_rows[:, t, :], low, ACT.Copy, scale=gi_signed[:, t : t + 1])
+        z2_codes = keep.tile([P, 512], U32, name="z2_codes", align_bytes=64)
+        z2_scales = keep.tile([P, 512], U8, name="z2_scales", align_bytes=64)
+        z2_grouped = []
+        for half in range(2):
+            grouped = keep.tile([P, 1024], BF16, name="z2_grouped%d" % half, tag="z_piece%d" % half, align_bytes=64)
+            nc.scalar.copy(
+                grouped[:].rearrange("p (c i t) -> p c t i", i=2, t=4),
+                z2_rows[:, :, 256 * half : 256 * (half + 1)].rearrange("p t (c i) -> p c t i", i=2),
             )
+            z2_grouped.append(grouped)
 
         z_codes = keep.tile([P, 512], U32, name="z_codes", align_bytes=64)
         z_scales = keep.tile([P, 512], U8, name="z_scales", align_bytes=64)
 
         for t in range(4):
-            gated = work("gated%d" % t)
-            nc.vector.tensor_tensor(gated[:], a_banks[t][:], sig1[t][:], ALU.mult)
-            this_g2 = g2
+            nc.vector.scalar_tensor_tensor(
+                gated[:, t, :], a_banks[t][:], gt_size[:, t : t + 1], sig1[t][:], ALU.mult, ALU.mult
+            )
             if t < 3:
-                g2 = a_gather(t + 1)
+                a_gather(t + 1)
             if t == 2:
-                z2_codes, z2_scales = quantize(z2_grouped, "z2")
-            larger = a_win[t + 1][:, 512:WINDOW] if t < 3 else b_win[0][:, 512:WINDOW]
-            nc.vector.tensor_tensor(larger, gated[:], this_g2[:], ALU.max)
-            gate_col = gates[:, 4 + t : 5 + t]
-            if t < 3:
-                nc.scalar.activation(
-                    z_grouped[:].rearrange("p (u m t) -> p m u t", u=4, t=4)[:, :, :, t],
-                    larger.rearrange("p (m u) -> p m u", u=4),
-                    ACT.Copy,
-                    scale=gate_col,
-                )
-            else:
-                for u in range(4):
-                    piece = z_grouped[:, 512 * u : 512 * (u + 1)]
-                    nc.scalar.activation(
-                        piece.rearrange("p (m t) -> p m t", t=4)[:, :, t],
-                        larger.rearrange("p (m u) -> p m u", u=4)[:, :, u],
-                        ACT.Copy,
-                        scale=gate_col,
+                for half in range(2):
+                    cols = slice(256 * half, 256 * (half + 1))
+                    nc.vector.quantize_mx(
+                        out=z2_codes[:, cols].bitcast(FP8X4), scales=z2_scales[:, cols], in_=z2_grouped[half][:]
                     )
-                    cols = slice(P * u, P * (u + 1))
-                    nc.vector.quantize_mx(out=z_codes[:, cols].bitcast(FP8X4), scales=z_scales[:, cols], in_=piece)
+        def quantize_z(u):
+            piece = keep.tile([P, 512], BF16, name="z_piece%d" % u, tag="z_piece%d" % (u % 2), align_bytes=64)
+            nc.vector.tensor_tensor(
+                piece[:].rearrange("p (g e t) -> p g t e", e=2, t=4),
+                gated[:].rearrange("p t (g u e) -> p u g t e", u=4, e=2)[:, u],
+                g2[:].rearrange("p t (g u e) -> p u g t e", u=4, e=2)[:, u],
+                ALU.max,
+            )
+            cols = slice(P * u, P * (u + 1))
+            nc.vector.quantize_mx(out=z_codes[:, cols].bitcast(FP8X4), scales=z_scales[:, cols], in_=piece[:])
 
-        out_rows = out.rearrange("(m u) n -> m u n", u=4)
+        for u in range(4):
+            quantize_z(u)
+
+        out_rows = out.rearrange("(g u e) n -> u e g n", u=4, e=2)
 
         def finish(u, first, second, tag):
             total = work("total%d" % u, tag)
             nc.vector.tensor_tensor(total[:], first[:], second[:], ALU.add)
-            nc.sync.dma_start(out_rows[:, u, :], total[:])
+            for e in range(2):
+                nc.sync.dma_start(out_rows[u, e], total[e:P:2, :])
 
         pending = None
         for u in range(4):
             bank = psum.tile([P, 512], F32, name="cv_bank%d" % u, tag="bank%d" % u)
             product(bank, z_codes, z_scales, u, z2_codes, z2_scales)
-            cv_win = keep.tile([P, WINDOW], F32, name="cv_win%d" % u)
+            cv_win = keep.tile([P, WINDOW], F32, name="cv_win%d" % u, tag="a_win%d" % u)
             nc.scalar.activation(cv_win[:, 0:512], bank[:], ACT.Copy, scale=0.0625)
             sig_here = work("sig_here%d" % u)
             nc.scalar.activation(sig_here[:], bank[:], ACT.Sigmoid, scale=0.0625)
@@ -245,4 +260,9 @@ def tile_picked_mombgmaxminmxwsum_none_p_kernel(
             second = work("second%d" % u)
             nc.vector.tensor_tensor(second[:], cv_win[:].indirect(n6_t[:]), sig7[:], ALU.mult)
             pending = (u, first, second)
-        finish(*pending, None)
+        last = work("total3")
+        for half in range(2):
+            cols = slice(256 * half, 256 * (half + 1))
+            nc.vector.tensor_tensor(last[:, cols], first[:, cols], second[:, cols], ALU.add)
+            for e, queue in enumerate((nc.scalar, nc.sync)):
+                queue.dma_start(out_rows[3, e][:, cols], last[e:P:2, cols])

@@ -70,18 +70,6 @@ def tile_picked_mombgmaxminmxwsum_none_p_kernel(
         n5_t = load_list(n5, "n5_t")
         n6_t = load_list(n6, "n6_t")
         n7_t = load_list(n7, "n7_t")
-        gate_ps = psum.tile([P, P], F32, name="gate_ps", tag="bank7")
-        nc.tensor.transpose(gate_ps[:], gate_rows[:, 0:P], identity[:])
-        gates = keep.tile([P, 8], F32, name="gates")
-        nc.scalar.activation(gates[:], gate_ps[:, 0:8], ACT.Copy)
-        gt_size = keep.tile([P, 4], F32, name="gt_size")
-        nc.scalar.activation(gt_size[:], gate_ps[:, 4:8], ACT.Abs)
-        gt_step = keep.tile([P, 4], F32, name="gt_step")
-        nc.gpsimd.tensor_scalar(gt_step[:], gates[:, 4:8], 0.0, 2.0, ALU.is_ge, ALU.mult)
-        gt_sign = keep.tile([P, 4], F32, name="gt_sign")
-        nc.gpsimd.tensor_scalar(gt_sign[:], gt_step[:], 1.0, -1.0, ALU.mult, ALU.add)
-        gi_signed = keep.tile([P, 4], F32, name="gi_signed")
-        nc.gpsimd.tensor_tensor(gi_signed[:], gates[:, 0:4], gt_sign[:], ALU.mult)
 
         def gather_words(lst, name):
             words = keep.tile([P, S], U32, name=name, align_bytes=64)
@@ -91,8 +79,8 @@ def tile_picked_mombgmaxminmxwsum_none_p_kernel(
             )
             return words
 
-        def gather_scales(lst, name):
-            listed = keep.tile([P, S], U8, name=name + "_listed")
+        def gather_scales(lst, name, tag):
+            listed = keep.tile([P, S], U8, name=name + "_listed", tag=tag, align_bytes=64)
             nc.vector.tensor_copy(listed[:], table_scales[:].indirect(lst[:]))
             return listed
 
@@ -105,18 +93,22 @@ def tile_picked_mombgmaxminmxwsum_none_p_kernel(
             return dealt
 
         def interleave_weight(raw, name):
-            grouped = keep.tile([P, PACK * 512], BF16, name=name, tag=name, align_bytes=64)
+            halves = []
             for half in range(2):
+                grouped = keep.tile([P, 1024], BF16, name="%s%d" % (name, half), align_bytes=64)
                 nc.scalar.copy(
-                    grouped[:, 1024 * half : 1024 * (half + 1)].rearrange("p (c i j) -> p c j i", i=2, j=PACK),
+                    grouped[:].rearrange("p (c i j) -> p c j i", i=2, j=PACK),
                     raw[half][:].rearrange("p j (c i) -> p c j i", i=2),
                 )
-            return grouped
+                halves.append(grouped)
+            return halves
 
-        def quantize(grouped, name):
+        def quantize(halves, name):
             codes = keep.tile([P, 512], U32, name=name + "_codes", align_bytes=64)
             scales = keep.tile([P, 512], U8, name=name + "_scales", align_bytes=64)
-            nc.vector.quantize_mx(out=codes[:].bitcast(FP8X4), scales=scales[:], in_=grouped[:])
+            for half in range(2):
+                cols = slice(256 * half, 256 * (half + 1))
+                nc.vector.quantize_mx(out=codes[:, cols].bitcast(FP8X4), scales=scales[:, cols], in_=halves[half][:])
             return codes, scales
 
         def product(bank, lhs_codes, lhs_scales, t, rhs_codes, rhs_scales):
@@ -134,8 +126,8 @@ def tile_picked_mombgmaxminmxwsum_none_p_kernel(
         def work(name, tag=None):
             return keep.tile([P, 512], F32, name=name, tag=tag or name, align_bytes=64)
 
-        xb_listed = gather_scales(two_t, "xb_scales")
-        xa_listed = gather_scales(offs_t, "xa_scales")
+        xb_listed = gather_scales(two_t, "xb_scales", "xb_listed")
+        xa_listed = gather_scales(offs_t, "xa_scales", "xa_listed")
         xb_scales = deal_scales(xb_listed, "xb_scales")
         xa_scales = deal_scales(xa_listed, "xa_scales")
         wb_grouped = interleave_weight(wb_raw, "wb_grouped")
@@ -144,30 +136,42 @@ def tile_picked_mombgmaxminmxwsum_none_p_kernel(
         xa_words = gather_words(offs_t, "xa_words")
 
         b_banks = [psum.tile([P, 512], F32, name="b_bank%d" % t, tag="bank%d" % t) for t in range(4)]
-        b_win = [keep.tile([P, WINDOW], F32, name="b_win%d" % t) for t in range(4)]
-        for t in range(4):
+        b_win = []
+        for t, tag in enumerate(("b_win0", "wa_raw0", "wa_raw1", "b_win3")):
+            b_win.append(keep.tile([P, WINDOW], F32, name="b_win%d" % t, tag=tag))
             product(b_banks[t], xb_words, xb_scales, t, wb_codes, wb_scales)
             nc.scalar.activation(b_win[t][:, 0:512], b_banks[t][:], ACT.Copy)
-            if t == 1:
+            if t == 0:
                 wa_grouped = interleave_weight(wa_raw, "wa_grouped")
 
         z2_rows = keep.tile([P, 4, 512], F32, name="z2_rows")
+        gate_ps = psum.tile([P, P], F32, name="gate_ps", tag="bank7")
+        nc.tensor.transpose(gate_ps[:], gate_rows[:, 0:P], identity[:])
+        gates = keep.tile([P, 8], F32, name="gates")
+        nc.scalar.activation(gates[:], gate_ps[:, 0:8], ACT.Copy)
+        gt_size = keep.tile([P, 4], F32, name="gt_size")
+        nc.scalar.activation(gt_size[:], gate_ps[:, 4:8], ACT.Abs)
+        gt_step = keep.tile([P, 4], F32, name="gt_step")
+        nc.gpsimd.tensor_scalar(gt_step[:], gates[:, 4:8], 0.0, 2.0, ALU.is_ge, ALU.mult)
+        gt_sign = keep.tile([P, 4], F32, name="gt_sign")
+        nc.gpsimd.tensor_scalar(gt_sign[:], gt_step[:], 1.0, -1.0, ALU.mult, ALU.add)
+        gi_signed = keep.tile([P, 4], F32, name="gi_signed")
+        nc.gpsimd.tensor_tensor(gi_signed[:], gates[:, 0:4], gt_sign[:], ALU.mult)
+
         a_banks = [psum.tile([P, 512], F32, name="a_bank%d" % t, tag="bank%d" % (4 + t)) for t in range(4)]
         a_win = [keep.tile([P, WINDOW], F32, name="a_win%d" % t) for t in range(4)]
         a_scaled = [keep.tile([P, WINDOW], F32, name="a_scaled%d" % t) for t in range(4)]
-        gated = keep.tile([P, 4, 512], F32, name="gated")
+        gated = keep.tile([P, 4, 512], F32, name="gated", align_bytes=64)
         g2 = keep.tile([P, 4, 512], F32, name="g2")
         sig1 = [work("sig1_%d" % t) for t in range(4)]
 
-        g3_tags = ["slot0", "wa_grouped", "slot1", "slot2"]
-        g4_tags = ["slot1", "slot2", "wa_grouped", "slot1"]
+        g3_tags = ["slot0", "wa_grouped0", "slot1", "slot2"]
+        g4_tags = ["slot1", "slot2", "wa_grouped0", "slot1"]
 
-        def b_gathers(t):
-            g3 = work("g3_%d" % t, g3_tags[t])
-            nc.vector.tensor_copy(g3[:], b_win[t][:].indirect(n3_t[:]))
-            g4 = work("g4_%d" % t, g4_tags[t])
-            nc.vector.tensor_copy(g4[:], b_win[t][:].indirect(n4_t[:]))
-            return g3, g4
+        def b_gather(lst, name, tag, t):
+            picked = work(name + "_%d" % t, tag)
+            nc.vector.tensor_copy(picked[:], b_win[t][:].indirect(lst[:]))
+            return picked
 
         def a_start(t):
             product(a_banks[t], xa_words, xa_scales, t, wa_codes, wa_scales)
@@ -178,25 +182,22 @@ def tile_picked_mombgmaxminmxwsum_none_p_kernel(
         def a_gather(t):
             nc.vector.tensor_copy(g2[:, t, :], a_scaled[t][:].indirect(n2_t[:]))
 
-        g3, g4 = b_gathers(0)
+        g3 = b_gather(n3_t, "g3", g3_tags[0], 0)
         for t in range(4):
+            g4 = b_gather(n4_t, "g4", g4_tags[t], t)
             upper = work("upper%d" % t)
             nc.vector.tensor_tensor(upper[:], b_banks[t][:], g3[:], ALU.max)
             if t == 0:
                 wa_codes, wa_scales = quantize(wa_grouped, "wa")
                 for s in range(4):
                     a_start(s)
-            this_g4 = g4
             if t < 3:
-                g3, g4 = b_gathers(t + 1)
-                low = b_win[t + 1][:, 512:WINDOW]
+                g3 = b_gather(n3_t, "g3", g3_tags[t + 1], t + 1)
             else:
                 a_gather(0)
-                low = a_scaled[0][:, 512:WINDOW]
-            nc.vector.tensor_tensor(low, upper[:], this_g4[:], ALU.min)
-            nc.scalar.activation(z2_rows[:, t, :], low, ACT.Copy, scale=gi_signed[:, t : t + 1])
-        z2_codes = keep.tile([P, 512], U32, name="z2_codes", align_bytes=64)
-        z2_scales = keep.tile([P, 512], U8, name="z2_scales", align_bytes=64)
+            low = work("low%d" % t, "wa_grouped1" if t == 0 else None)
+            nc.vector.tensor_tensor(low[:], upper[:], g4[:], ALU.min)
+            nc.scalar.activation(z2_rows[:, t, :], low[:], ACT.Copy, scale=gi_signed[:, t : t + 1])
         z2_grouped = []
         for half in range(2):
             grouped = keep.tile([P, 1024], BF16, name="z2_grouped%d" % half, tag="z_piece%d" % half, align_bytes=64)
@@ -216,11 +217,8 @@ def tile_picked_mombgmaxminmxwsum_none_p_kernel(
             if t < 3:
                 a_gather(t + 1)
             if t == 2:
-                for half in range(2):
-                    cols = slice(256 * half, 256 * (half + 1))
-                    nc.vector.quantize_mx(
-                        out=z2_codes[:, cols].bitcast(FP8X4), scales=z2_scales[:, cols], in_=z2_grouped[half][:]
-                    )
+                z2_codes, z2_scales = quantize(z2_grouped, "z2")
+
         def quantize_z(u):
             piece = keep.tile([P, 512], BF16, name="z_piece%d" % u, tag="z_piece%d" % (u % 2), align_bytes=64)
             nc.vector.tensor_tensor(
@@ -253,12 +251,12 @@ def tile_picked_mombgmaxminmxwsum_none_p_kernel(
             nc.scalar.activation(sig_here[:], bank[:], ACT.Sigmoid, scale=0.0625)
             sig7 = work("sig7_%d" % u)
             nc.scalar.activation(sig7[:], cv_win[:].indirect(n7_t[:]), ACT.Sigmoid)
-            first = work("first%d" % u)
+            first = work("first%d" % u, "gated" if u == 0 else None)
             nc.vector.tensor_tensor(first[:], cv_win[:].indirect(n5_t[:]), sig_here[:], ALU.mult)
-            if pending:
-                finish(*pending, "sig_here%d" % u)
             second = work("second%d" % u)
             nc.vector.tensor_tensor(second[:], cv_win[:].indirect(n6_t[:]), sig7[:], ALU.mult)
+            if pending:
+                finish(*pending, "sig_here%d" % u)
             pending = (u, first, second)
         last = work("total3")
         for half in range(2):

@@ -178,6 +178,7 @@ def tile_picked_mombgmaxminmxwsum_none_p_kernel(
             nc.scalar.activation(a_scaled[t][:, 0:512], a_banks[t][:], ACT.Copy, scale=gt_size[:, t : t + 1])
             nc.scalar.activation(a_win[t][:, 0:512], a_banks[t][:], ACT.Copy)
             nc.scalar.activation(sig1[t][:], a_win[t][:].indirect(n1_t[:]), ACT.Sigmoid)
+            nc.gpsimd.tensor_tensor(gated[:, t, :], a_scaled[t][:, 0:512], sig1[t][:], ALU.mult)
 
         def a_gather(t):
             nc.vector.tensor_copy(g2[:, t, :], a_scaled[t][:].indirect(n2_t[:]))
@@ -211,9 +212,6 @@ def tile_picked_mombgmaxminmxwsum_none_p_kernel(
         z_scales = keep.tile([P, 512], U8, name="z_scales", align_bytes=64)
 
         for t in range(4):
-            nc.vector.scalar_tensor_tensor(
-                gated[:, t, :], a_banks[t][:], gt_size[:, t : t + 1], sig1[t][:], ALU.mult, ALU.mult
-            )
             if t < 3:
                 a_gather(t + 1)
             if t == 2:
@@ -251,7 +249,7 @@ def tile_picked_mombgmaxminmxwsum_none_p_kernel(
             nc.scalar.activation(sig_here[:], bank[:], ACT.Sigmoid, scale=0.0625)
             sig7 = work("sig7_%d" % u)
             nc.scalar.activation(sig7[:], cv_win[:].indirect(n7_t[:]), ACT.Sigmoid)
-            first = work("first%d" % u, "gated" if u == 0 else None)
+            first = work("first%d" % u)
             nc.vector.tensor_tensor(first[:], cv_win[:].indirect(n5_t[:]), sig_here[:], ALU.mult)
             second = work("second%d" % u)
             nc.vector.tensor_tensor(second[:], cv_win[:].indirect(n6_t[:]), sig7[:], ALU.mult)

from contextlib import ExitStack

import concourse.mybir as mybir
from concourse.masks import make_identity

K, T, S, H, N = 512, 2048, 512, 512, 512
FLOPS = 3 * 2 * 512 * 512 * 512

F32 = mybir.dt.float32
BF16 = mybir.dt.bfloat16
I32 = mybir.dt.int32
U32 = mybir.dt.uint32
U16 = mybir.dt.uint16
U8 = mybir.dt.uint8
FP8X4 = mybir.dt.float8_e4m3fn_x4
ALU = mybir.AluOpType
ACT = mybir.ActivationFunctionType

P = 128
PACK = 4
WINDOW = 1024


def tile_picked_mombgmaxminmxwsum_none_p_kernel(
    tc, x_words, x_scales, wa, wb, gt, gi, offs, two, n1, n2, n3, n4, n5, n6, n7, out
):
    nc = tc.nc
    with ExitStack() as ctx:
        keep = ctx.enter_context(tc.tile_pool(name="keep", bufs=1))
        psum = ctx.enter_context(tc.psum_pool(name="psum", bufs=1))

        def load_list(src, name):
            tile = keep.tile([P, S // 16], U16, name=name)
            nc.sync.dma_start(tile[:], src)
            return tile

        def load_weight_half(w, half, name):
            tile = keep.tile([P, PACK, 256], F32, name=name)
            nc.sync.dma_start(tile[:], w.rearrange("(p j) c -> p j c", j=PACK)[:, :, 256 * half : 256 * (half + 1)])
            return tile

        table_scales = keep.tile([P, T], U8, name="table_scales")
        nc.gpsimd.memset(table_scales[:].bitcast(I32), 0)
        gate_rows = keep.tile([P, P + 8], F32, name="gate_rows")
        nc.gpsimd.memset(gate_rows[:], 0.0)
        identity = keep.tile([P, P], F32, name="identity")
        make_identity(nc, identity[:])

        warm = keep.tile([P, 1], F32, name="warm")
        two_t = load_list(two, "two_t")
        offs_t = load_list(offs, "offs_t")
        for q in range(4):
            nc.scalar.dma_start(
                table_scales[32 * q : 32 * q + 4, :].bitcast(I32), x_scales[0, 4 * q : 4 * q + 4, :].bitcast(I32)
            )
        nc.scalar.activation(warm[:], gate_rows[:, P : P + 1], ACT.Sigmoid)
        wb_raw = [load_weight_half(wb, half, "wb_raw%d" % half) for half in range(2)]
        table_words = keep.tile([P, T], I32, name="table_words")
        nc.sync.dma_start(table_words[:], x_words[0].rearrange("p n t -> p (n t)").bitcast(I32))
        n3_t = load_list(n3, "n3_t")
        n4_t = load_list(n4, "n4_t")
        for row, gate in ((0, gi), (4, gt)):
            nc.sync.dma_start(
                gate_rows[row : row + 4, 0:P].rearrange("t (g e) -> t g e", e=4),
                gate.rearrange("(g t e) o -> t g (e o)", t=4, e=4),
            )
        wa_raw = [load_weight_half(wa, half, "wa_raw%d" % half) for half in range(2)]
        n1_t = load_list(n1, "n1_t")
        n2_t = load_list(n2, "n2_t")
        n5_t = load_list(n5, "n5_t")
        n6_t = load_list(n6, "n6_t")
        n7_t = load_list(n7, "n7_t")

        def gather_words(lst, name):
            words = keep.tile([P, S], U32, name=name, align_bytes=64)
            nc.vector.tensor_copy(
                words[:].rearrange("p (t g e) -> p g t e", t=4, e=4),
                table_words[:].bitcast(U32).indirect(lst[:]),
            )
            return words

        def gather_scales(lst, name, tag):
            listed = keep.tile([P, S], U8, name=name + "_listed", tag=tag, align_bytes=64)
            nc.vector.tensor_copy(listed[:], table_scales[:].indirect(lst[:]))
            return listed

        def deal_scales(listed, name):
            dealt = keep.tile([P, S], U8, name=name, align_bytes=64)
            nc.vector.tensor_copy(
                dealt[:].bitcast(I32).rearrange("p (t g) -> p t g", t=4),
                listed[:].bitcast(I32).rearrange("p (g t) -> p t g", t=4),
            )
            return dealt

        def interleave_weight(raw, name):
            halves = []
            for half in range(2):
                grouped = keep.tile([P, 1024], BF16, name="%s%d" % (name, half), align_bytes=64)
                nc.scalar.copy(
                    grouped[:].rearrange("p (c i j) -> p c j i", i=2, j=PACK),
                    raw[half][:].rearrange("p j (c i) -> p c j i", i=2),
                )
                halves.append(grouped)
            return halves

        def quantize(halves, name):
            codes = keep.tile([P, 512], U32, name=name + "_codes", align_bytes=64)
            scales = keep.tile([P, 512], U8, name=name + "_scales", align_bytes=64)
            for half in range(2):
                cols = slice(256 * half, 256 * (half + 1))
                nc.vector.quantize_mx(out=codes[:, cols].bitcast(FP8X4), scales=scales[:, cols], in_=halves[half][:])
            return codes, scales

        def product(bank, lhs_codes, lhs_scales, t, rhs_codes, rhs_scales):
            cols = slice(P * t, P * (t + 1))
            nc.tensor.matmul_mx(
                out=bank[:],
                lhsT=lhs_codes[:, cols].bitcast(FP8X4),
                lhsT_scale=lhs_scales[:, cols],
                rhs=rhs_codes[:].bitcast(FP8X4),
                rhs_scale=rhs_scales[:],
                start=True,
                stop=True,
            )

        def work(name, tag=None):
            return keep.tile([P, 512], F32, name=name, tag=tag or name, align_bytes=64)

        xb_listed = gather_scales(two_t, "xb_scales", "xb_listed")
        xa_listed = gather_scales(offs_t, "xa_scales", "xa_listed")
        xb_scales = deal_scales(xb_listed, "xb_scales")
        xa_scales = deal_scales(xa_listed, "xa_scales")
        wb_grouped = interleave_weight(wb_raw, "wb_grouped")
        wb_codes, wb_scales = quantize(wb_grouped, "wb")
        xb_words = gather_words(two_t, "xb_words")
        xa_words = gather_words(offs_t, "xa_words")

        b_banks = [psum.tile([P, 512], F32, name="b_bank%d" % t, tag="bank%d" % t) for t in range(4)]
        b_win = []
        for t, tag in enumerate(("b_win0", "wa_raw0", "wa_raw1", "b_win3")):
            b_win.append(keep.tile([P, WINDOW], F32, name="b_win%d" % t, tag=tag))
            product(b_banks[t], xb_words, xb_scales, t, wb_codes, wb_scales)
            nc.scalar.activation(b_win[t][:, 0:512], b_banks[t][:], ACT.Copy)
            if t == 0:
                wa_grouped = interleave_weight(wa_raw, "wa_grouped")

        z2_rows = keep.tile([P, 4, 512], F32, name="z2_rows")
        gate_ps = psum.tile([P, P], F32, name="gate_ps", tag="bank7")
        nc.tensor.transpose(gate_ps[:], gate_rows[:, 0:P], identity[:])
        gates = keep.tile([P, 8], F32, name="gates")
        nc.scalar.activation(gates[:], gate_ps[:, 0:8], ACT.Copy)
        gt_size = keep.tile([P, 4], F32, name="gt_size")
        nc.scalar.activation(gt_size[:], gate_ps[:, 4:8], ACT.Abs)
        gt_step = keep.tile([P, 4], F32, name="gt_step")
        nc.gpsimd.tensor_scalar(gt_step[:], gates[:, 4:8], 0.0, 2.0, ALU.is_ge, ALU.mult)
        gt_sign = keep.tile([P, 4], F32, name="gt_sign")
        nc.gpsimd.tensor_scalar(gt_sign[:], gt_step[:], 1.0, -1.0, ALU.mult, ALU.add)
        gi_signed = keep.tile([P, 4], F32, name="gi_signed")
        nc.gpsimd.tensor_tensor(gi_signed[:], gates[:, 0:4], gt_sign[:], ALU.mult)

        a_banks = [psum.tile([P, 512], F32, name="a_bank%d" % t, tag="bank%d" % (4 + t)) for t in range(4)]
        a_win = [keep.tile([P, WINDOW], F32, name="a_win%d" % t) for t in range(4)]
        a_scaled = [keep.tile([P, WINDOW], F32, name="a_scaled%d" % t) for t in range(4)]
        gated = keep.tile([P, 4, 512], F32, name="gated", align_bytes=64)
        g2 = keep.tile([P, 4, 512], F32, name="g2")
        sig1 = [work("sig1_%d" % t) for t in range(4)]

        g3_tags = ["slot0", "wa_grouped0", "slot1", "slot2"]
        g4_tags = ["slot1", "slot2", "wa_grouped0", "slot1"]

        def b_gather(lst, name, tag, t):
            picked = work(name + "_%d" % t, tag)
            nc.vector.tensor_copy(picked[:], b_win[t][:].indirect(lst[:]))
            return picked

        def a_start(t):
            product(a_banks[t], xa_words, xa_scales, t, wa_codes, wa_scales)
            nc.scalar.activation(a_scaled[t][:, 0:512], a_banks[t][:], ACT.Copy, scale=gt_size[:, t : t + 1])
            nc.scalar.activation(a_win[t][:, 0:512], a_banks[t][:], ACT.Copy)
            nc.scalar.activation(sig1[t][:], a_win[t][:].indirect(n1_t[:]), ACT.Sigmoid)
            nc.gpsimd.tensor_tensor(gated[:, t, :], a_scaled[t][:, 0:512], sig1[t][:], ALU.mult)

        def a_gather(t):
            nc.vector.tensor_copy(g2[:, t, :], a_scaled[t][:].indirect(n2_t[:]))

        g3 = b_gather(n3_t, "g3", g3_tags[0], 0)
        for t in range(4):
            g4 = b_gather(n4_t, "g4", g4_tags[t], t)
            upper = work("upper%d" % t)
            nc.vector.tensor_tensor(upper[:], b_banks[t][:], g3[:], ALU.max)
            if t == 0:
                wa_codes, wa_scales = quantize(wa_grouped, "wa")
                for s in range(4):
                    a_start(s)
            if t < 3:
                g3 = b_gather(n3_t, "g3", g3_tags[t + 1], t + 1)
            else:
                a_gather(0)
            low = work("low%d" % t, "wa_grouped1" if t == 0 else None)
            nc.vector.tensor_tensor(low[:], upper[:], g4[:], ALU.min)
            nc.scalar.activation(z2_rows[:, t, :], low[:], ACT.Copy, scale=gi_signed[:, t : t + 1])
        z2_grouped = []
        for half in range(2):
            grouped = keep.tile([P, 1024], BF16, name="z2_grouped%d" % half, tag="z_piece%d" % half, align_bytes=64)
            nc.scalar.copy(
                grouped[:].rearrange("p (c i t) -> p c t i", i=2, t=4),
                z2_rows[:, :, 256 * half : 256 * (half + 1)].rearrange("p t (c i) -> p c t i", i=2),
            )
            z2_grouped.append(grouped)

        z_codes = keep.tile([P, 512], U32, name="z_codes", align_bytes=64)
        z_scales = keep.tile([P, 512], U8, name="z_scales", align_bytes=64)

        for t in range(4):
            if t < 3:
                a_gather(t + 1)
            if t == 2:
                z2_codes, z2_scales = quantize(z2_grouped, "z2")

        def quantize_z(u):
            piece = keep.tile([P, 512], BF16, name="z_piece%d" % u, tag="z_piece%d" % (u % 2), align_bytes=64)
            nc.vector.tensor_tensor(
                piece[:].rearrange("p (g e t) -> p g t e", e=2, t=4),
                gated[:].rearrange("p t (g u e) -> p u g t e", u=4, e=2)[:, u],
                g2[:].rearrange("p t (g u e) -> p u g t e", u=4, e=2)[:, u],
                ALU.max,
            )
            cols = slice(P * u, P * (u + 1))
            nc.vector.quantize_mx(out=z_codes[:, cols].bitcast(FP8X4), scales=z_scales[:, cols], in_=piece[:])

        for u in range(4):
            quantize_z(u)

        out_rows = out.rearrange("(g u e) n -> u e g n", u=4, e=2)

        def finish(u, first, second, tag):
            total = work("total%d" % u, tag)
            nc.vector.tensor_tensor(total[:], first[:], second[:], ALU.add)
            for e in range(2):
                nc.sync.dma_start(out_rows[u, e], total[e:P:2, :])

        pending = None
        for u in range(4):
            bank = psum.tile([P, 512], F32, name="cv_bank%d" % u, tag="bank%d" % u)
            product(bank, z_codes, z_scales, u, z2_codes, z2_scales)
            cv_win = keep.tile([P, WINDOW], F32, name="cv_win%d" % u, tag="a_win%d" % u)
            nc.scalar.activation(cv_win[:, 0:512], bank[:], ACT.Copy, scale=0.0625)
            sig_here = work("sig_here%d" % u)
            nc.scalar.activation(sig_here[:], bank[:], ACT.Sigmoid, scale=0.0625)
            sig7 = work("sig7_%d" % u)
            nc.scalar.activation(sig7[:], cv_win[:].indirect(n7_t[:]), ACT.Sigmoid)
            first = work("first%d" % u)
            nc.vector.tensor_tensor(first[:], cv_win[:].indirect(n5_t[:]), sig_here[:], ALU.mult)
            second = work("second%d" % u)
            nc.vector.tensor_tensor(second[:], cv_win[:].indirect(n6_t[:]), sig7[:], ALU.mult)
            if pending:
                finish(*pending, "sig_here%d" % u)
            pending = (u, first, second)
        last = work("total3")
        for half in range(2):
            cols = slice(256 * half, 256 * (half + 1))
            nc.vector.tensor_tensor(last[:, cols], first[:, cols], second[:, cols], ALU.add)
            for e, queue in enumerate((nc.scalar, nc.sync)):
                queue.dma_start(out_rows[3, e][:, cols], last[e:P:2, cols])
